import numpy as np
import ml_dtypes

BF16 = ml_dtypes.bfloat16


def bf(x):
    return np.asarray(x, np.float32).astype(BF16)


def f32(x):
    return np.asarray(x, np.float32)


def f64(x):
    return np.asarray(x).astype(np.float64)


def striped(idx):
    return np.tile(idx.reshape(-1, 16).T, (8, 1))


S, K, M, N, E, Q = 512, 256, 256, 192, 2, 96


def setup_inputs():
    return {"base": bf(np.random.standard_normal((M, S))), "x": bf(np.random.standard_normal((K, N))), "w": bf(np.random.standard_normal((E, K, M)) / np.sqrt(K)), "s": f32(0.5 + np.random.random_sample((M, 1))), "b": f32(0.5 * np.random.standard_normal((M, 1))), "offs": striped(np.random.permutation(S)[:N])}


def reference(base, x, w, s, b, offs):
    idx = offs[:16].T.reshape(-1)
    z = f64(base).copy()
    for e in range(E):
        z[:, idx[e * Q : (e + 1) * Q]] += f64(w)[e].T @ f64(x)[:, e * Q : (e + 1) * Q]
    return z * f64(s) + f64(b)

@@ -1,0 +1,61 @@
+import concourse.mybir as mybir
+from concourse.masks import make_identity
+
+BF16, F32, U16 = mybir.dt.bfloat16, mybir.dt.float32, mybir.dt.uint16
+P = 128
+FLOPS = 2 * 256 * 256 * 192
+
+
+def tile_scatter_matmul_kernel(tc, base, x, w, s, b, offs, out):
+    nc = tc.nc
+    rows, slots = base.shape
+    contraction, entries = x.shape
+    experts = w.shape[0]
+    windows = rows // P
+    blocks = contraction // P
+    piece = entries // experts
+    piece_cols = piece // 16
+
+    with (
+        tc.tile_pool(name="held", bufs=1) as held,
+        tc.psum_pool(name="psum", bufs=1) as psum,
+    ):
+        offsets = held.tile([P, entries // 16], U16, name="offsets")
+        base_t = held.tile([P, windows, slots], BF16, name="base_t")
+        x_t = held.tile([P, blocks, entries], BF16, name="x_t")
+        w_t = held.tile([P, experts, blocks, rows], BF16, name="w_t")
+        gain = held.tile([P, windows], F32, name="gain")
+        shift = held.tile([P, windows], F32, name="shift")
+        ident = held.tile([P, P], BF16, name="ident")
+
+        nc.sync.dma_start(base_t[:], base.rearrange("(a p) t -> p a t", p=P))
+        nc.sync.dma_start(offsets[:], offs)
+        nc.sync.dma_start(x_t[:], x.rearrange("(p c) n -> p c n", p=P))
+        nc.sync.dma_start(w_t[:], w.rearrange("e (p c) m -> p e c m", p=P))
+        nc.sync.dma_start(gain[:], s.rearrange("(a p) o -> p (a o)", p=P))
+        nc.sync.dma_start(shift[:], b.rearrange("(a p) o -> p (a o)", p=P))
+        make_identity(nc, ident[:])
+
+        banks = [psum.tile([P, slots], F32, name=f"window{a}") for a in range(windows)]
+        for a in range(windows):
+            nc.tensor.matmul(banks[a][:], ident[:], base_t[:, a, :], start=True, stop=False)
+
+        for a in range(windows):
+            for e in range(experts):
+                places = banks[a][:].indirect(offsets[:, e * piece_cols : (e + 1) * piece_cols])
+                for c in range(blocks):
+                    nc.tensor.matmul(
+                        places,
+                        w_t[:, e, c, a * P : (a + 1) * P],
+                        x_t[:, c, e * piece : (e + 1) * piece],
+                        start=False,
+                        stop=(e == experts - 1 and c == blocks - 1),
+                    )
+
+        for a in range(windows):
+            result = held.tile([P, slots], F32, name=f"result{a}")
+            nc.vector.tensor_scalar(
+                result[:], banks[a][:], gain[:, a : a + 1], shift[:, a : a + 1],
+                op0=mybir.AluOpType.mult, op1=mybir.AluOpType.add,
+            )
+            nc.sync.dma_start(out[a * P : (a + 1) * P, :], result[:])

@@ -3,6 +3,7 @@ from concourse.masks import make_identity
 
 BF16, F32, U16 = mybir.dt.bfloat16, mybir.dt.float32, mybir.dt.uint16
 P = 128
+WARM_UPS = 4
 FLOPS = 2 * 256 * 256 * 192
 
 
@@ -35,6 +36,12 @@ def tile_scatter_matmul_kernel(tc, base, x, w, s, b, offs, out):
         nc.sync.dma_start(gain[:], s.rearrange("(a p) o -> p (a o)", p=P))
         nc.sync.dma_start(shift[:], b.rearrange("(a p) o -> p (a o)", p=P))
         make_identity(nc, ident[:])
+
+        zeros = held.tile([P, slots], BF16, name="zeros")
+        nc.vector.memset(zeros[:], 0.0)
+        unread = psum.tile([P, slots], F32, name="unread")
+        for i in range(WARM_UPS):
+            nc.tensor.matmul(unread[:], zeros[:, :P], zeros[:], start=True, stop=True)
 
         banks = [psum.tile([P, slots], F32, name=f"window{a}") for a in range(windows)]
         for a in range(windows):

@@ -29,12 +29,12 @@ def tile_scatter_matmul_kernel(tc, base, x, w, s, b, offs, out):
         shift = held.tile([P, windows], F32, name="shift")
         ident = held.tile([P, P], BF16, name="ident")
 
-        nc.sync.dma_start(base_t[:], base.rearrange("(a p) t -> p a t", p=P))
+        nc.sync.dma_start(base_t[:], base.rearrange("(p a) t -> p a t", p=P))
         nc.sync.dma_start(offsets[:], offs)
         nc.sync.dma_start(x_t[:], x.rearrange("(p c) n -> p c n", p=P))
         nc.sync.dma_start(w_t[:], w.rearrange("e (p c) m -> p e c m", p=P))
-        nc.sync.dma_start(gain[:], s.rearrange("(a p) o -> p (a o)", p=P))
-        nc.sync.dma_start(shift[:], b.rearrange("(a p) o -> p (a o)", p=P))
+        nc.sync.dma_start(gain[:], s.rearrange("(p a) o -> p (a o)", p=P))
+        nc.sync.dma_start(shift[:], b.rearrange("(p a) o -> p (a o)", p=P))
         make_identity(nc, ident[:])
 
         zeros = held.tile([P, slots], BF16, name="zeros")
@@ -53,16 +53,17 @@ def tile_scatter_matmul_kernel(tc, base, x, w, s, b, offs, out):
                 for c in range(blocks):
                     nc.tensor.matmul(
                         places,
-                        w_t[:, e, c, a * P : (a + 1) * P],
+                        w_t[:, e, c, a::windows],
                         x_t[:, c, e * piece : (e + 1) * piece],
                         start=False,
                         stop=(e == experts - 1 and c == blocks - 1),
                     )
 
+        out_rows = out.rearrange("(p a) t -> p a t", p=P)
         for a in range(windows):
             result = held.tile([P, slots], F32, name=f"result{a}")
             nc.vector.tensor_scalar(
                 result[:], banks[a][:], gain[:, a : a + 1], shift[:, a : a + 1],
                 op0=mybir.AluOpType.mult, op1=mybir.AluOpType.add,
             )
-            nc.sync.dma_start(out[a * P : (a + 1) * P, :], result[:])
+            nc.sync.dma_start(out_rows[:, a, :], result[:])

@@ -3,7 +3,8 @@ from concourse.masks import make_identity
 
 BF16, F32, U16 = mybir.dt.bfloat16, mybir.dt.float32, mybir.dt.uint16
 P = 128
-WARM_UPS = 4
+WARM_UPS = 6
+WARM_COLS = 256
 FLOPS = 2 * 256 * 256 * 192
 
 
@@ -37,9 +38,9 @@ def tile_scatter_matmul_kernel(tc, base, x, w, s, b, offs, out):
         nc.sync.dma_start(shift[:], b.rearrange("(p a) o -> p (a o)", p=P))
         make_identity(nc, ident[:])
 
-        zeros = held.tile([P, slots], BF16, name="zeros")
+        zeros = held.tile([P, WARM_COLS], BF16, name="zeros")
         nc.vector.memset(zeros[:], 0.0)
-        unread = psum.tile([P, slots], F32, name="unread")
+        unread = psum.tile([P, WARM_COLS], F32, name="unread")
         for i in range(WARM_UPS):
             nc.tensor.matmul(unread[:], zeros[:, :P], zeros[:], start=True, stop=True)
 

import concourse.mybir as mybir
from concourse.masks import make_identity

BF16, F32, U16 = mybir.dt.bfloat16, mybir.dt.float32, mybir.dt.uint16
P = 128
WARM_UPS = 6
WARM_COLS = 256
FLOPS = 2 * 256 * 256 * 192


def tile_scatter_matmul_kernel(tc, base, x, w, s, b, offs, out):
    nc = tc.nc
    rows, slots = base.shape
    contraction, entries = x.shape
    experts = w.shape[0]
    windows = rows // P
    blocks = contraction // P
    piece = entries // experts
    piece_cols = piece // 16

    with (
        tc.tile_pool(name="held", bufs=1) as held,
        tc.psum_pool(name="psum", bufs=1) as psum,
    ):
        offsets = held.tile([P, entries // 16], U16, name="offsets")
        base_t = held.tile([P, windows, slots], BF16, name="base_t")
        x_t = held.tile([P, blocks, entries], BF16, name="x_t")
        w_t = held.tile([P, experts, blocks, rows], BF16, name="w_t")
        gain = held.tile([P, windows], F32, name="gain")
        shift = held.tile([P, windows], F32, name="shift")
        ident = held.tile([P, P], BF16, name="ident")

        nc.sync.dma_start(base_t[:], base.rearrange("(p a) t -> p a t", p=P))
        nc.sync.dma_start(offsets[:], offs)
        nc.sync.dma_start(x_t[:], x.rearrange("(p c) n -> p c n", p=P))
        nc.sync.dma_start(w_t[:], w.rearrange("e (p c) m -> p e c m", p=P))
        nc.sync.dma_start(gain[:], s.rearrange("(p a) o -> p (a o)", p=P))
        nc.sync.dma_start(shift[:], b.rearrange("(p a) o -> p (a o)", p=P))
        make_identity(nc, ident[:])

        zeros = held.tile([P, WARM_COLS], BF16, name="zeros")
        nc.vector.memset(zeros[:], 0.0)
        unread = psum.tile([P, WARM_COLS], F32, name="unread")
        for i in range(WARM_UPS):
            nc.tensor.matmul(unread[:], zeros[:, :P], zeros[:], start=True, stop=True)

        banks = [psum.tile([P, slots], F32, name=f"window{a}") for a in range(windows)]
        for a in range(windows):
            nc.tensor.matmul(banks[a][:], ident[:], base_t[:, a, :], start=True, stop=False)

        for a in range(windows):
            for e in range(experts):
                places = banks[a][:].indirect(offsets[:, e * piece_cols : (e + 1) * piece_cols])
                for c in range(blocks):
                    nc.tensor.matmul(
                        places,
                        w_t[:, e, c, a::windows],
                        x_t[:, c, e * piece : (e + 1) * piece],
                        start=False,
                        stop=(e == experts - 1 and c == blocks - 1),
                    )

        out_rows = out.rearrange("(p a) t -> p a t", p=P)
        for a in range(windows):
            result = held.tile([P, slots], F32, name=f"result{a}")
            nc.vector.tensor_scalar(
                result[:], banks[a][:], gain[:, a : a + 1], shift[:, a : a + 1],
                op0=mybir.AluOpType.mult, op1=mybir.AluOpType.add,
            )
            nc.sync.dma_start(out_rows[:, a, :], result[:])
